import numpy as np
import ml_dtypes


def mxq(x, axis, fmt="e4m3"):
    dtype, down = {"e4m3": (ml_dtypes.float8_e4m3fn, 7), "e5m2": (ml_dtypes.float8_e5m2, 14)}[fmt]
    v = np.moveaxis(np.asarray(x, np.float32).astype(ml_dtypes.bfloat16).astype(np.float64), axis, -1)
    blocks = v.reshape(v.shape[:-1] + (-1, 32))
    amax = np.abs(blocks).max(-1, keepdims=True)
    byte = np.maximum(np.where(amax > 0, np.frexp(amax)[1] - 1 + 127, 0) - down, 1)
    scale = np.exp2(byte - 127.0)
    codes = (blocks / scale).astype(np.float32).astype(dtype).astype(np.float64)
    return np.moveaxis((codes * scale).reshape(v.shape), -1, axis)


WIDE = False


def mx_kscale(k):
    if not WIDE:
        return np.ones(k)
    levels = np.array([10, -10, 5, -5, 0])
    if k % 512:
        return np.exp2(np.random.permutation(np.resize(levels, k // 32))).repeat(32)
    a = np.empty((k // 512, 16))
    for p in range(k // 512):
        a[p, :8] = np.random.permutation(np.resize(levels, 8))
        for g in range(8):
            far = levels[np.abs(levels - a[p, g]) >= 10]
            a[p, g + 8] = far[np.random.randint(len(far))]
    return np.exp2(a.ravel()).repeat(32)


def f64(x):
    return np.asarray(x).astype(np.float64)


def striped(idx):
    return np.tile(idx.reshape(-1, 16).T, (8, 1)).astype(np.uint16)


def unstriped(offs):
    return offs[:16].T.reshape(-1).astype(np.int64)


def striped8(idx):
    return np.concatenate([x.reshape(-1, 16).T for x in idx]).astype(np.uint16)


def runs(offs, k):
    lists = np.stack([offs[16 * r : 16 * r + 16].T.reshape(-1) for r in range(8)]).astype(np.int64)
    return lists[np.arange(k) % 512 // 64]


def pack_weight(w):
    k, n = w.shape
    w = f64(np.asarray(w, np.float32).astype(ml_dtypes.bfloat16)).reshape(k // 32, 32, n)
    amax = np.abs(w).max(1)
    byte = np.clip(np.where(amax > 0, np.frexp(amax)[1] - 1 + 127 - 7, 1), 1, 254)
    scaled = (w * np.exp2(127.0 - byte)[:, None, :]).reshape(k, n).astype(np.float32)
    words = np.ascontiguousarray(scaled.reshape(k // 512, 128, 4, n).transpose(0, 1, 3, 2)).astype(ml_dtypes.float8_e4m3fn).view(np.uint8)
    return words, np.ascontiguousarray(byte.astype(np.uint8).reshape(k // 512, 16, n))


def unpack_weight(words, scales):
    g, p, n, _ = words.shape
    vals = np.ascontiguousarray(words).view(ml_dtypes.float8_e4m3fn).astype(np.float64) * np.repeat(np.exp2(scales.astype(np.float64) - 127.0), 8, axis=1)[..., None]
    return vals.transpose(0, 1, 3, 2).reshape(g * 512, n)


def sigmoid(v):
    return 1.0 / (1.0 + np.exp(-np.maximum(v, -700.0)))

def planes(y):
    n, m = y.shape
    v = y.astype(np.float32).astype(ml_dtypes.bfloat16).astype(np.float64).reshape(n // 32, 32, m)
    top = np.abs(v).max(1)
    byte = np.clip(np.where(top > 0, np.frexp(top)[1] - 1 + 127 - 7, 1), 1, 254)
    codes = (v * np.exp2(127.0 - byte)[:, None, :]).reshape(n, m).astype(np.float32).astype(ml_dtypes.float8_e4m3fn).view(np.uint8)
    words = codes.reshape(n // 512, 128, 4, m).transpose(0, 1, 3, 2)
    return np.ascontiguousarray(words), np.ascontiguousarray(byte.astype(np.uint8).reshape(n // 512, 16, m))


K, T, S, V, H = 512, 2048, 512, 256, 512


def setup_inputs():
    n = np.random.standard_normal
    s = mx_kscale(K)[:, None]
    u = mx_kscale(S)
    packed_xT = pack_weight(n((K, T)) * s)
    packed_w1 = pack_weight(n((K, H)) / np.sqrt(K) / s)
    packed_w2 = pack_weight(n((K, H)) / np.sqrt(K) / s)
    packed_w3 = pack_weight(n((K, H)) / np.sqrt(K) / s)
    return {
        "x_words": packed_xT[0],
        "x_scales": packed_xT[1],
        "w1_words": packed_w1[0],
        "w1_scales": packed_w1[1],
        "w2_words": packed_w2[0],
        "w2_scales": packed_w2[1],
        "w3_words": packed_w3[0],
        "w3_scales": packed_w3[1],
        "ga": (np.random.uniform(0.5, 1.5, (H, 1)) * u[:, None]).astype(np.float32),
        "gb": (np.random.uniform(0.5, 1.5, (H, 1)) / u[:, None]).astype(np.float32),
        "offs": striped(np.random.permutation(T)[:S]),
        "two": striped(np.random.permutation(T)[:S]),
        "n1": striped(np.random.permutation(S)),
        "n2": striped(np.random.permutation(S)),
        "three": striped(np.random.permutation(T)[:V]),
        "n3": striped8(np.stack([np.random.permutation(V) for _ in range(8)])),
        "n4": striped8(np.stack([np.random.permutation(V) for _ in range(8)])),
        "n5": striped8(np.stack([np.random.permutation(V) for _ in range(8)])),
    }


def reference(x_words, x_scales, w1_words, w1_scales, w2_words, w2_scales, w3_words, w3_scales, ga, gb, offs, two, n1, n2, three, n3, n4, n5):
    xq = unpack_weight(x_words, x_scales)[:, unstriped(offs)]
    y = unpack_weight(w1_words, w1_scales).T @ xq
    x_two = unpack_weight(x_words, x_scales)[:, unstriped(two)]
    d = unpack_weight(w2_words, w2_scales).T @ x_two
    z = f64(ga) * ((y + y[:, unstriped(n1)]) * (sigmoid(d + d[:, unstriped(n2)])))
    x_three = unpack_weight(x_words, x_scales)[:, unstriped(three)]
    b = unpack_weight(w3_words, w3_scales).T @ x_three
    z2 = f64(gb) * (np.maximum(b, b[np.arange(H)[:, None], runs(n3, H)]))
    s = 0.0625 * ((mxq(z, 0, "e4m3").T @ mxq(z2, 0, "e4m3")))
    pa = s[np.arange(S)[:, None], runs(n4, S)]
    pb = s[np.arange(S)[:, None], runs(n5, S)]
    mu = 0.3125 * (s + pa + pb)
    out_0 = (s - mu) / (np.sqrt((pa - mu) ** 2 + (pb - mu) ** 2 + 0.25))
    return (out_0,) + planes(out_0)

@@ -1,0 +1,308 @@
+from contextlib import ExitStack
+
+import concourse.mybir as mybir
+
+K, T, S, V, H = 512, 2048, 512, 256, 512
+P = 128
+F32 = mybir.dt.float32
+BF16 = mybir.dt.bfloat16
+I32 = mybir.dt.int32
+U32 = mybir.dt.uint32
+U16 = mybir.dt.uint16
+U8 = mybir.dt.uint8
+FP8X4 = mybir.dt.float8_e4m3fn_x4
+ACT = mybir.ActivationFunctionType
+ALU = mybir.AluOpType
+
+FLOPS = 2 * K * H * (S + S + V) + 2 * H * S * V
+
+
+def tile_picked_twktriebbigstd_none_po_kernel(
+    tc, x_words, x_scales, w1_words, w1_scales, w2_words, w2_scales, w3_words, w3_scales,
+    ga, gb, offs, two, n1, n2, three, n3, n4, n5, out_0, out_1, out_2,
+):
+    nc = tc.nc
+    with ExitStack() as ctx:
+        sb = ctx.enter_context(tc.tile_pool(name="sb", bufs=1))
+        ps = ctx.enter_context(tc.psum_pool(name="ps", bufs=1))
+
+        def tile(name, shape, dtype):
+            return sb.tile(shape, dtype, name=name, align_bytes=64)
+
+        def bank(name, number):
+            return ps.tile([P, 512], F32, name=name, tag="bank%d" % number)
+
+        def load_list(name, src):
+            t = tile(name, list(src.shape), U16)
+            nc.sync.dma_start(t[:], src)
+            return t
+
+        def load_words(name, src, cols):
+            t = tile(name, [P, cols], U32)
+            nc.sync.dma_start(t[:].bitcast(I32), src[0].rearrange("p n r -> p (n r)").bitcast(I32))
+            return t
+
+        def load_scales(t, src):
+            for q in range(4):
+                nc.sync.dma_start(t[32 * q : 32 * q + 4, :].bitcast(I32), src[0][4 * q : 4 * q + 4, :].bitcast(I32))
+
+        def load_gain(name, src):
+            t = tile(name, [P, 4], F32)
+            by_b = src.rearrange("(h t b) o -> b h (t o)", t=4, b=4)
+            with nc.allow_non_contiguous_dma(reason="one value for each feature"):
+                for b in range(4):
+                    nc.sync.dma_start(t[b:P:4, :], by_b[b])
+            return t
+
+        xs = tile("xs", [P, T], U8)
+        nc.vector.memset(xs[:].bitcast(I32), 0)
+        ws_raw = {}
+        for w in (3, 2, 1):
+            ws_raw[w] = tile("ws_raw%d" % w, [P, H], U8)
+            nc.vector.memset(ws_raw[w][:].bitcast(I32), 0)
+        win = [tile("win%d" % t, [P, 2 * V], F32) for t in range(4)]
+        d_win = [tile("d_win%d" % t, [P, S + 16], F32) for t in range(4)]
+        for t in range(4):
+            nc.vector.memset(win[t][:, V:], 0.0)
+        for t in range(4):
+            nc.vector.memset(d_win[t][:, S:], 0.0)
+
+        ww_raw = {}
+        l_three = load_list("l_three", three)
+        ww_raw[3] = load_words("ww_raw3", w3_words, H)
+        l_two = load_list("l_two", two)
+        load_scales(xs, x_scales)
+        xw = load_words("xw", x_words, T)
+        load_scales(ws_raw[3], w3_scales)
+        ww_raw[2] = load_words("ww_raw2", w2_words, H)
+        l_offs = load_list("l_offs", offs)
+        load_scales(ws_raw[2], w2_scales)
+        l_n3 = load_list("l_n3", n3)
+        ww_raw[1] = load_words("ww_raw1", w1_words, H)
+        load_scales(ws_raw[1], w1_scales)
+        ga_t = load_gain("ga_t", ga)
+        l_n2 = load_list("l_n2", n2)
+        l_n1 = load_list("l_n1", n1)
+        gb_t = load_gain("gb_t", gb)
+        l_n4 = load_list("l_n4", n4)
+        l_n5 = load_list("l_n5", n5)
+
+        def deal(w, move):
+            words = tile("ww%d" % w, [P, H], U32)
+            move(
+                words[:].rearrange("p (t h b) -> p t h b", t=4, b=4),
+                ww_raw[w][:].rearrange("p (h t b) -> p t h b", t=4, b=4),
+            )
+            scales = tile("ws%d" % w, [P, H], U8)
+            move(
+                scales[:].bitcast(U32).rearrange("p (t h) -> p t h", t=4),
+                ws_raw[w][:].bitcast(U32).rearrange("p (h t) -> p t h", t=4),
+            )
+            return words, scales
+
+        def pick_scales(name, lst, n):
+            t = tile(name, [P, n], U8)
+            nc.vector.tensor_copy(t[:], xs[:].indirect(lst[:]))
+            return t
+
+        def pick_words(name, lst, n):
+            t = tile(name, [P, n], U32)
+            nc.vector.tensor_copy(t[:], xw[:].indirect(lst[:]))
+            return t
+
+        def product(out, lhs, t, rhs):
+            cols = slice(P * t, P * (t + 1))
+            nc.tensor.matmul_mx(
+                out=out, lhsT=lhs[0][:, cols].bitcast(FP8X4), lhsT_scale=lhs[1][:, cols],
+                rhs=rhs[0][:].bitcast(FP8X4), rhs_scale=rhs[1][:], start=True, stop=True,
+            )
+
+        def fetch(out, window, lst, lo, hi):
+            nc.scalar.activation(out, window[:].indirect(lst[:, lo // 16 : hi // 16]), ACT.Copy)
+
+        s3 = pick_scales("s3", l_three, V)
+        s2 = pick_scales("s2", l_two, S)
+        w3 = deal(3, nc.scalar.copy)
+        x3 = (pick_words("x3", l_three, V), s3)
+        x2 = (pick_words("x2", l_two, S), s2)
+
+        p_b = [bank("p_b%d" % t, 4 + t) for t in range(4)]
+        for t in range(4):
+            product(p_b[t][:, :V], w3, t, x3)
+        w2 = deal(2, nc.gpsimd.tensor_copy)
+        b_got = tile("b_got", [P, 4, V], F32)
+        for t in range(4):
+            nc.scalar.copy(win[t][:, :V], p_b[t][:, :V])
+            fetch(b_got[:, t, :], win[t], l_n3, 0, V)
+
+        p_d = [bank("p_d%d" % t, t) for t in range(4)]
+        for t in range(4):
+            product(p_d[t][:], w2, t, x2)
+        d_got = [tile("d_got%d" % t, [P, S], F32) for t in range(4)]
+        nc.vector.tensor_copy(d_win[0][:, :S], p_d[0][:])
+        x1 = (pick_words("x1", l_offs, S), pick_scales("s1", l_offs, S))
+        w1 = deal(1, nc.gpsimd.tensor_copy)
+        for t in range(1, 4):
+            nc.vector.tensor_copy(d_win[t][:, :S], p_d[t][:])
+        p_y = [bank("p_y%d" % t, 4 + t) for t in range(4)]
+        for t in range(4):
+            product(p_y[t][:], w1, t, x1)
+
+        d_sum = tile("d_sum", [P, 4, S], F32)
+        gate = tile("gate", [P, 4, S], F32)
+        y_sum = tile("y_sum", [P, 4, S], F32)
+        y_win = [tile("y_win%d" % t, [P, S], F32) for t in range(4)]
+        b_max = tile("b_max", [P, 4, V], F32)
+
+        for t in range(4):
+            if t < 0:
+                nc.scalar.activation(y_win[t][:], p_y[t][:], ACT.Copy, scale=ga_t[:, t : t + 1])
+            else:
+                nc.vector.tensor_scalar(y_win[t][:], p_y[t][:], ga_t[:, t : t + 1], None, ALU.mult)
+        for t in range(4):
+            nc.vector.tensor_tensor(b_max[:, t, :], win[t][:, :V], b_got[:, t, :], ALU.max)
+        z2_bf = tile("z2_bf", [P, V * 4], BF16)
+        nc.vector.tensor_tensor(
+            z2_bf[:].rearrange("p (c i t) -> p c t i", i=4, t=4),
+            b_max[:].rearrange("p t (c i) -> p c t i", i=4),
+            gb_t[:].rearrange("p (c t i) -> p c t i", c=1, i=1).to_broadcast([P, V // 4, 4, 4]),
+            ALU.mult,
+        )
+        for t in range(4):
+            fetch(d_got[t][:], d_win[t], l_n2, 0, S)
+            nc.vector.tensor_tensor(d_sum[:, t, :], p_d[t][:], d_got[t][:], ALU.add)
+        z2q = (tile("z2_words", [P, V], U32), tile("z2_scales", [P, V], U8))
+        nc.vector.quantize_mx(out=z2q[0][:].bitcast(FP8X4), scales=z2q[1][:], in_=z2_bf[:])
+        for t in range(4):
+            nc.scalar.activation(gate[:, t, :], d_sum[:, t, :], ACT.Sigmoid)
+
+        zq = (tile("z_words", [P, S], U32), tile("z_scales", [P, S], U8))
+        z_bf = [tile("z_bf%d" % h, [P, 4 * 64 * 4], BF16) for h in range(2)]
+
+        def y_fetch(lo, hi):
+            for t in range(4):
+                y_got = sb.tile([P, hi - lo], F32, name="y_got", tag="y_got%d" % t, align_bytes=64)
+                fetch(y_got[:], y_win[t], l_n1, lo, hi)
+                nc.vector.scalar_tensor_tensor(
+                    y_sum[:, t, lo:hi], p_y[t][:, lo:hi], ga_t[:, t : t + 1], y_got[:], ALU.mult, ALU.add
+                )
+            return y_got
+
+        def z_make(lo, hi):
+            h, m0, m1 = lo // 256, lo % 256 // 4, (hi - 1) % 256 // 4 + 1
+            nc.vector.tensor_tensor(
+                z_bf[h][:].rearrange("p (r m t) -> p m t r", r=4, t=4)[:, m0:m1],
+                y_sum[:, :, lo:hi].rearrange("p t (m r) -> p m t r", r=4),
+                gate[:, :, lo:hi].rearrange("p t (m r) -> p m t r", r=4),
+                ALU.mult,
+            )
+
+        def z_quantize(h, r):
+            cols = slice(P * r + 64 * h, P * r + 64 * (h + 1))
+            nc.vector.quantize_mx(
+                out=zq[0][:, cols].bitcast(FP8X4), scales=zq[1][:, cols], in_=z_bf[h][:, 256 * r : 256 * (r + 1)]
+            )
+
+        cuts = (0, 128, 256, 384, 512)
+        for lo, hi in zip(cuts, cuts[1:]):
+            y_last = y_fetch(lo, hi)
+            z_make(lo, hi)
+            if lo == 256:
+                for r in range(4):
+                    z_quantize(0, r)
+        p_s = [bank("p_s%d" % r, r) for r in range(4)]
+        for r in range(4):
+            z_quantize(1, r)
+            product(p_s[r][:, :V], zq, r, z2q)
+        for r in range(4):
+            nc.vector.tensor_scalar(win[r][:, :V], p_s[r][:, :V], 0.0625, None, ALU.mult)
+
+        out_words = tile("out_words", [P, V], U32)
+        out_scales = tile("out_scales", [P, V], U8)
+        out_rows = out_0.rearrange("(p r) v -> p r v", r=4)
+        res = tile("res", [P, 4, V], F32)
+        rounded = tile("rounded", [P, 4 * V], BF16)
+        pieces = [(r, 0, V) for r in range(4)]
+        held = {}
+
+        def stage_fetch(k):
+            r, lo, hi = pieces[k]
+            pa = tile("pa%d" % k, [P, hi - lo], F32)
+            pb = tile("pb%d" % k, [P, hi - lo], F32)
+            fetch(pa[:], win[r], l_n4, lo, hi)
+            fetch(pb[:], win[r], l_n5, lo, hi)
+            held[k] = [pa, pb]
+
+        def stage_linear(k):
+            r, lo, hi = pieces[k]
+            pa, pb = held[k]
+            raw = p_s[r][:, lo:hi]
+            both = tile("both%d" % k, [P, hi - lo], F32)
+            fg = tile("fg%d" % k, [P, 2, hi - lo], F32)
+            num = tile("num%d" % k, [P, hi - lo], F32)
+            nc.vector.tensor_tensor(both[:], pa[:], pb[:], ALU.add)
+            nc.vector.tensor_tensor(fg[:, 0], pa[:], pb[:], ALU.subtract)
+            nc.vector.scalar_tensor_tensor(fg[:, 1], both[:], -9.6, raw, ALU.mult, ALU.add)
+            nc.vector.scalar_tensor_tensor(num[:], both[:], -80.0 / 11.0, raw, ALU.mult, ALU.add)
+            held[k] = [fg, num]
+
+        def stage_square(k):
+            fg, num = held[k]
+            sq = tile("sq%d" % k, list(fg.shape), F32)
+            if k in ():
+                nc.vector.tensor_tensor(sq[:], fg[:], fg[:], ALU.mult)
+            else:
+                nc.scalar.activation(sq[:], fg[:], ACT.Square)
+            held[k] = [sq, num]
+
+        def stage_sum(k):
+            sq, num = held[k]
+            q = tile("q%d" % k, list(num.shape), F32)
+            nc.vector.scalar_tensor_tensor(q[:], sq[:, 1], 0.390625 / 256.0, sq[:, 0], ALU.mult, ALU.add)
+            held[k] = [q, num]
+
+        def stage_root(k):
+            q, num = held[k]
+            inv = tile("inv%d" % k, list(num.shape), F32)
+            nc.scalar.activation(inv[:], q[:], ACT.Abs_reciprocal_sqrt, bias=0.25, scale=0.5)
+            held[k] = [inv, num]
+
+        def stage_out(k):
+            r, lo, hi = pieces[k]
+            inv, num = held[k]
+            nc.vector.scalar_tensor_tensor(res[:, r, lo:hi], num[:], 0.6875 / 16.0, inv[:], ALU.mult, ALU.mult)
+            nc.sync.dma_start(out_rows[:, r, lo:hi], res[:, r, lo:hi])
+
+        def stage_round(k):
+            r, lo, hi = pieces[k]
+            if r == 3:
+                nc.vector.tensor_copy(
+                    rounded[:, 4 * lo : 4 * hi].rearrange("p (c i r) -> p c r i", i=4, r=4),
+                    res[:, :, lo:hi].rearrange("p r (c i) -> p c r i", i=4),
+                )
+
+        def stage_planes(k):
+            r, lo, hi = pieces[k]
+            if r == 3:
+                nc.vector.quantize_mx(
+                    out=out_words[:, lo:hi].bitcast(FP8X4), scales=out_scales[:, lo:hi], in_=rounded[:, 4 * lo : 4 * hi]
+                )
+                nc.sync.dma_start(
+                    out_1[0].rearrange("p c r -> p (c r)").bitcast(I32)[:, lo:hi], out_words[:, lo:hi].bitcast(I32)
+                )
+
+        for k in range(len(pieces)):
+            stage_fetch(k)
+        for k in range(len(pieces)):
+            stage_linear(k)
+        stages = [stage_square, stage_sum, stage_root, stage_out, stage_round, stage_planes]
+        for step in range(len(pieces) + len(stages) - 1):
+            for depth in reversed(range(len(stages))):
+                k = step - depth
+                if 0 <= k < len(pieces):
+                    stages[depth](k)
+        for q in range(4):
+            engine = nc.scalar if q % 2 else nc.sync
+            engine.dma_start(
+                out_2[0][4 * q : 4 * q + 4, :].bitcast(I32), out_scales[32 * q : 32 * q + 4, :].bitcast(I32)
+            )

@@ -120,6 +120,9 @@ def tile_picked_twktriebbigstd_none_po_kernel(
         def fetch(out, window, lst, lo, hi):
             nc.scalar.activation(out, window[:].indirect(lst[:, lo // 16 : hi // 16]), ACT.Copy)
 
+        warm = tile("warm", [P, 2], F32)
+        nc.gpsimd.memset(warm[:, 0:1], 1.0)
+        nc.scalar.activation(warm[:, 1:2], warm[:, 0:1], ACT.Sigmoid)
         s3 = pick_scales("s3", l_three, V)
         s2 = pick_scales("s2", l_two, S)
         w3 = deal(3, nc.scalar.copy)
@@ -210,6 +213,7 @@ def tile_picked_twktriebbigstd_none_po_kernel(
             if lo == 256:
                 for r in range(4):
                     z_quantize(0, r)
+        nc.scalar.activation(warm[:, 0:1], y_last[:, 0:1], ACT.Abs_reciprocal_sqrt, bias=0.25, scale=0.5)
         p_s = [bank("p_s%d" % r, r) for r in range(4)]
         for r in range(4):
             z_quantize(1, r)

@@ -1,6 +1,7 @@
 from contextlib import ExitStack
 
 import concourse.mybir as mybir
+from concourse.masks import make_identity
 
 K, T, S, V, H = 512, 2048, 512, 256, 512
 P = 128
@@ -82,8 +83,8 @@ def tile_picked_twktriebbigstd_none_po_kernel(
         load_scales(ws_raw[1], w1_scales)
         ga_t = load_gain("ga_t", ga)
         l_n2 = load_list("l_n2", n2)
-        l_n1 = load_list("l_n1", n1)
         gb_t = load_gain("gb_t", gb)
+        l_n1 = load_list("l_n1", n1)
         l_n4 = load_list("l_n4", n4)
         l_n5 = load_list("l_n5", n5)
 
@@ -123,6 +124,8 @@ def tile_picked_twktriebbigstd_none_po_kernel(
         warm = tile("warm", [P, 2], F32)
         nc.gpsimd.memset(warm[:, 0:1], 1.0)
         nc.scalar.activation(warm[:, 1:2], warm[:, 0:1], ACT.Sigmoid)
+        ident = tile("ident", [P, P], F32)
+        make_identity(nc, ident[:])
         s3 = pick_scales("s3", l_three, V)
         s2 = pick_scales("s2", l_two, S)
         w3 = deal(3, nc.scalar.copy)
@@ -135,7 +138,8 @@ def tile_picked_twktriebbigstd_none_po_kernel(
         w2 = deal(2, nc.gpsimd.tensor_copy)
         b_got = tile("b_got", [P, 4, V], F32)
         for t in range(4):
-            nc.scalar.copy(win[t][:, :V], p_b[t][:, :V])
+            move = nc.scalar.copy if t < 4 else nc.vector.tensor_copy
+            move(win[t][:, :V], p_b[t][:, :V])
             fetch(b_got[:, t, :], win[t], l_n3, 0, V)
 
         p_d = [bank("p_d%d" % t, t) for t in range(4)]
@@ -151,8 +155,8 @@ def tile_picked_twktriebbigstd_none_po_kernel(
         for t in range(4):
             product(p_y[t][:], w1, t, x1)
 
-        d_sum = tile("d_sum", [P, 4, S], F32)
-        gate = tile("gate", [P, 4, S], F32)
+        p_sum = [bank("p_sum%d" % c, c) for c in range(4)]
+        gate_t = [tile("gate_t%d" % c, [P, H], F32) for c in range(4)]
         y_sum = tile("y_sum", [P, 4, S], F32)
         y_win = [tile("y_win%d" % t, [P, S], F32) for t in range(4)]
         b_max = tile("b_max", [P, 4, V], F32)
@@ -173,11 +177,20 @@ def tile_picked_twktriebbigstd_none_po_kernel(
         )
         for t in range(4):
             fetch(d_got[t][:], d_win[t], l_n2, 0, S)
-            nc.vector.tensor_tensor(d_sum[:, t, :], p_d[t][:], d_got[t][:], ALU.add)
+            for c in range(4):
+                cols = slice(P * c, P * (c + 1))
+                out = p_sum[c][:, P * t : P * (t + 1)]
+                nc.tensor.matmul(out, d_got[t][:, cols], ident[:], start=True, stop=False, is_transpose=True)
+                nc.tensor.matmul(out, d_win[t][:, cols], ident[:], start=False, stop=True, is_transpose=True)
         z2q = (tile("z2_words", [P, V], U32), tile("z2_scales", [P, V], U8))
         nc.vector.quantize_mx(out=z2q[0][:].bitcast(FP8X4), scales=z2q[1][:], in_=z2_bf[:])
-        for t in range(4):
-            nc.scalar.activation(gate[:, t, :], d_sum[:, t, :], ACT.Sigmoid)
+        p_gate = [bank("p_gate%d" % c, 4 + c) for c in range(4)]
+
+        def make_gate(c):
+            nc.scalar.activation(gate_t[c][:], p_sum[c][:], ACT.Sigmoid)
+            for t in range(4):
+                cols = slice(P * t, P * (t + 1))
+                nc.tensor.transpose(p_gate[c][:, cols], gate_t[c][:, cols], ident[:])
 
         zq = (tile("z_words", [P, S], U32), tile("z_scales", [P, S], U8))
         z_bf = [tile("z_bf%d" % h, [P, 4 * 64 * 4], BF16) for h in range(2)]
@@ -186,17 +199,15 @@ def tile_picked_twktriebbigstd_none_po_kernel(
             for t in range(4):
                 y_got = sb.tile([P, hi - lo], F32, name="y_got", tag="y_got%d" % t, align_bytes=64)
                 fetch(y_got[:], y_win[t], l_n1, lo, hi)
-                nc.vector.scalar_tensor_tensor(
-                    y_sum[:, t, lo:hi], p_y[t][:, lo:hi], ga_t[:, t : t + 1], y_got[:], ALU.mult, ALU.add
-                )
+                nc.vector.tensor_tensor(y_sum[:, t, lo:hi], y_win[t][:, lo:hi], y_got[:], ALU.add)
             return y_got
 
-        def z_make(lo, hi):
-            h, m0, m1 = lo // 256, lo % 256 // 4, (hi - 1) % 256 // 4 + 1
+        def z_make(c, r0, r1):
+            h, m0 = c // 2, c % 2 * 32
             nc.vector.tensor_tensor(
-                z_bf[h][:].rearrange("p (r m t) -> p m t r", r=4, t=4)[:, m0:m1],
-                y_sum[:, :, lo:hi].rearrange("p t (m r) -> p m t r", r=4),
-                gate[:, :, lo:hi].rearrange("p t (m r) -> p m t r", r=4),
+                z_bf[h][:].rearrange("p (r m t) -> p m t r", r=4, t=4)[:, m0 : m0 + 32, :, r0:r1],
+                y_sum[:, :, P * c : P * (c + 1)].rearrange("p t (m r) -> p m t r", r=4)[:, :, :, r0:r1],
+                p_gate[c][:].rearrange("p (t m r) -> p m t r", t=4, r=4)[:, :, :, r0:r1],
                 ALU.mult,
             )
 
@@ -206,13 +217,19 @@ def tile_picked_twktriebbigstd_none_po_kernel(
                 out=zq[0][:, cols].bitcast(FP8X4), scales=zq[1][:, cols], in_=z_bf[h][:, 256 * r : 256 * (r + 1)]
             )
 
-        cuts = (0, 128, 256, 384, 512)
+        for c in range(4):
+            make_gate(c)
+        cuts = (0,256,384,512)
         for lo, hi in zip(cuts, cuts[1:]):
             y_last = y_fetch(lo, hi)
-            z_make(lo, hi)
-            if lo == 256:
-                for r in range(4):
-                    z_quantize(0, r)
+            for c in range(lo // P, hi // P):
+                if c < 3:
+                    z_make(c, 0, 4)
+                if c == 2:
+                    for r in range(4):
+                        z_quantize(0, r)
+        z_make(3, 0, 2)
+        z_make(3, 2, 4)
         nc.scalar.activation(warm[:, 0:1], y_last[:, 0:1], ACT.Abs_reciprocal_sqrt, bias=0.25, scale=0.5)
         p_s = [bank("p_s%d" % r, r) for r in range(4)]
         for r in range(4):

@@ -61,6 +61,8 @@ def tile_picked_twktriebbigstd_none_po_kernel(
         for w in (3, 2, 1):
             ws_raw[w] = tile("ws_raw%d" % w, [P, H], U8)
             nc.vector.memset(ws_raw[w][:].bitcast(I32), 0)
+        ident = tile("ident", [P, P], F32)
+        nc.vector.memset(ident[:], 0.0)
         win = [tile("win%d" % t, [P, 2 * V], F32) for t in range(4)]
         d_win = [tile("d_win%d" % t, [P, S + 16], F32) for t in range(4)]
         for t in range(4):
@@ -79,13 +81,13 @@ def tile_picked_twktriebbigstd_none_po_kernel(
         l_offs = load_list("l_offs", offs)
         load_scales(ws_raw[2], w2_scales)
         l_n3 = load_list("l_n3", n3)
+        ga_t = load_gain("ga_t", ga)
         ww_raw[1] = load_words("ww_raw1", w1_words, H)
         load_scales(ws_raw[1], w1_scales)
-        ga_t = load_gain("ga_t", ga)
+        l_n4 = load_list("l_n4", n4)
         l_n2 = load_list("l_n2", n2)
         gb_t = load_gain("gb_t", gb)
         l_n1 = load_list("l_n1", n1)
-        l_n4 = load_list("l_n4", n4)
         l_n5 = load_list("l_n5", n5)
 
         def deal(w, move):
@@ -122,10 +124,8 @@ def tile_picked_twktriebbigstd_none_po_kernel(
             nc.scalar.activation(out, window[:].indirect(lst[:, lo // 16 : hi // 16]), ACT.Copy)
 
         warm = tile("warm", [P, 2], F32)
-        nc.gpsimd.memset(warm[:, 0:1], 1.0)
-        nc.scalar.activation(warm[:, 1:2], warm[:, 0:1], ACT.Sigmoid)
-        ident = tile("ident", [P, P], F32)
-        make_identity(nc, ident[:])
+        nc.scalar.activation(warm[:, 1:2], ident[:, 0:1], ACT.Sigmoid)
+        make_identity(nc, ident[:], nomemset=True)
         s3 = pick_scales("s3", l_three, V)
         s2 = pick_scales("s2", l_two, S)
         w3 = deal(3, nc.scalar.copy)
@@ -135,7 +135,7 @@ def tile_picked_twktriebbigstd_none_po_kernel(
         p_b = [bank("p_b%d" % t, 4 + t) for t in range(4)]
         for t in range(4):
             product(p_b[t][:, :V], w3, t, x3)
-        w2 = deal(2, nc.gpsimd.tensor_copy)
+        w2 = (ww_raw[2], ws_raw[2])
         b_got = tile("b_got", [P, 4, V], F32)
         for t in range(4):
             move = nc.scalar.copy if t < 4 else nc.vector.tensor_copy
@@ -187,7 +187,11 @@ def tile_picked_twktriebbigstd_none_po_kernel(
         p_gate = [bank("p_gate%d" % c, 4 + c) for c in range(4)]
 
         def make_gate(c):
-            nc.scalar.activation(gate_t[c][:], p_sum[c][:], ACT.Sigmoid)
+            nc.scalar.activation(
+                gate_t[c][:].rearrange("p (t h b) -> p h t b", t=4, b=4),
+                p_sum[c][:].rearrange("p (h t b) -> p h t b", t=4, b=4),
+                ACT.Sigmoid,
+            )
             for t in range(4):
                 cols = slice(P * t, P * (t + 1))
                 nc.tensor.transpose(p_gate[c][:, cols], gate_t[c][:, cols], ident[:])

from contextlib import ExitStack

import concourse.mybir as mybir
from concourse.masks import make_identity

K, T, S, V, H = 512, 2048, 512, 256, 512
P = 128
F32 = mybir.dt.float32
BF16 = mybir.dt.bfloat16
I32 = mybir.dt.int32
U32 = mybir.dt.uint32
U16 = mybir.dt.uint16
U8 = mybir.dt.uint8
FP8X4 = mybir.dt.float8_e4m3fn_x4
ACT = mybir.ActivationFunctionType
ALU = mybir.AluOpType

FLOPS = 2 * K * H * (S + S + V) + 2 * H * S * V


def tile_picked_twktriebbigstd_none_po_kernel(
    tc, x_words, x_scales, w1_words, w1_scales, w2_words, w2_scales, w3_words, w3_scales,
    ga, gb, offs, two, n1, n2, three, n3, n4, n5, out_0, out_1, out_2,
):
    nc = tc.nc
    with ExitStack() as ctx:
        sb = ctx.enter_context(tc.tile_pool(name="sb", bufs=1))
        ps = ctx.enter_context(tc.psum_pool(name="ps", bufs=1))

        def tile(name, shape, dtype):
            return sb.tile(shape, dtype, name=name, align_bytes=64)

        def bank(name, number):
            return ps.tile([P, 512], F32, name=name, tag="bank%d" % number)

        def load_list(name, src):
            t = tile(name, list(src.shape), U16)
            nc.sync.dma_start(t[:], src)
            return t

        def load_words(name, src, cols):
            t = tile(name, [P, cols], U32)
            nc.sync.dma_start(t[:].bitcast(I32), src[0].rearrange("p n r -> p (n r)").bitcast(I32))
            return t

        def load_scales(t, src):
            for q in range(4):
                nc.sync.dma_start(t[32 * q : 32 * q + 4, :].bitcast(I32), src[0][4 * q : 4 * q + 4, :].bitcast(I32))

        def load_gain(name, src):
            t = tile(name, [P, 4], F32)
            by_b = src.rearrange("(h t b) o -> b h (t o)", t=4, b=4)
            with nc.allow_non_contiguous_dma(reason="one value for each feature"):
                for b in range(4):
                    nc.sync.dma_start(t[b:P:4, :], by_b[b])
            return t

        xs = tile("xs", [P, T], U8)
        nc.vector.memset(xs[:].bitcast(I32), 0)
        ws_raw = {}
        for w in (3, 2, 1):
            ws_raw[w] = tile("ws_raw%d" % w, [P, H], U8)
            nc.vector.memset(ws_raw[w][:].bitcast(I32), 0)
        ident = tile("ident", [P, P], F32)
        nc.vector.memset(ident[:], 0.0)
        win = [tile("win%d" % t, [P, 2 * V], F32) for t in range(4)]
        d_win = [tile("d_win%d" % t, [P, S + 16], F32) for t in range(4)]
        for t in range(4):
            nc.vector.memset(win[t][:, V:], 0.0)
        for t in range(4):
            nc.vector.memset(d_win[t][:, S:], 0.0)

        ww_raw = {}
        l_three = load_list("l_three", three)
        ww_raw[3] = load_words("ww_raw3", w3_words, H)
        l_two = load_list("l_two", two)
        load_scales(xs, x_scales)
        xw = load_words("xw", x_words, T)
        load_scales(ws_raw[3], w3_scales)
        ww_raw[2] = load_words("ww_raw2", w2_words, H)
        l_offs = load_list("l_offs", offs)
        load_scales(ws_raw[2], w2_scales)
        l_n3 = load_list("l_n3", n3)
        ga_t = load_gain("ga_t", ga)
        ww_raw[1] = load_words("ww_raw1", w1_words, H)
        load_scales(ws_raw[1], w1_scales)
        l_n4 = load_list("l_n4", n4)
        l_n2 = load_list("l_n2", n2)
        gb_t = load_gain("gb_t", gb)
        l_n1 = load_list("l_n1", n1)
        l_n5 = load_list("l_n5", n5)

        def deal(w, move):
            words = tile("ww%d" % w, [P, H], U32)
            move(
                words[:].rearrange("p (t h b) -> p t h b", t=4, b=4),
                ww_raw[w][:].rearrange("p (h t b) -> p t h b", t=4, b=4),
            )
            scales = tile("ws%d" % w, [P, H], U8)
            move(
                scales[:].bitcast(U32).rearrange("p (t h) -> p t h", t=4),
                ws_raw[w][:].bitcast(U32).rearrange("p (h t) -> p t h", t=4),
            )
            return words, scales

        def pick_scales(name, lst, n):
            t = tile(name, [P, n], U8)
            nc.vector.tensor_copy(t[:], xs[:].indirect(lst[:]))
            return t

        def pick_words(name, lst, n):
            t = tile(name, [P, n], U32)
            nc.vector.tensor_copy(t[:], xw[:].indirect(lst[:]))
            return t

        def product(out, lhs, t, rhs):
            cols = slice(P * t, P * (t + 1))
            nc.tensor.matmul_mx(
                out=out, lhsT=lhs[0][:, cols].bitcast(FP8X4), lhsT_scale=lhs[1][:, cols],
                rhs=rhs[0][:].bitcast(FP8X4), rhs_scale=rhs[1][:], start=True, stop=True,
            )

        def fetch(out, window, lst, lo, hi):
            nc.scalar.activation(out, window[:].indirect(lst[:, lo // 16 : hi // 16]), ACT.Copy)

        warm = tile("warm", [P, 2], F32)
        nc.scalar.activation(warm[:, 1:2], ident[:, 0:1], ACT.Sigmoid)
        make_identity(nc, ident[:], nomemset=True)
        s3 = pick_scales("s3", l_three, V)
        s2 = pick_scales("s2", l_two, S)
        w3 = deal(3, nc.scalar.copy)
        x3 = (pick_words("x3", l_three, V), s3)
        x2 = (pick_words("x2", l_two, S), s2)

        p_b = [bank("p_b%d" % t, 4 + t) for t in range(4)]
        for t in range(4):
            product(p_b[t][:, :V], w3, t, x3)
        w2 = (ww_raw[2], ws_raw[2])
        b_got = tile("b_got", [P, 4, V], F32)
        for t in range(4):
            move = nc.scalar.copy if t < 4 else nc.vector.tensor_copy
            move(win[t][:, :V], p_b[t][:, :V])
            fetch(b_got[:, t, :], win[t], l_n3, 0, V)

        p_d = [bank("p_d%d" % t, t) for t in range(4)]
        for t in range(4):
            product(p_d[t][:], w2, t, x2)
        d_got = [tile("d_got%d" % t, [P, S], F32) for t in range(4)]
        nc.vector.tensor_copy(d_win[0][:, :S], p_d[0][:])
        x1 = (pick_words("x1", l_offs, S), pick_scales("s1", l_offs, S))
        w1 = deal(1, nc.gpsimd.tensor_copy)
        for t in range(1, 4):
            nc.vector.tensor_copy(d_win[t][:, :S], p_d[t][:])
        p_y = [bank("p_y%d" % t, 4 + t) for t in range(4)]
        for t in range(4):
            product(p_y[t][:], w1, t, x1)

        p_sum = [bank("p_sum%d" % c, c) for c in range(4)]
        gate_t = [tile("gate_t%d" % c, [P, H], F32) for c in range(4)]
        y_sum = tile("y_sum", [P, 4, S], F32)
        y_win = [tile("y_win%d" % t, [P, S], F32) for t in range(4)]
        b_max = tile("b_max", [P, 4, V], F32)

        for t in range(4):
            if t < 0:
                nc.scalar.activation(y_win[t][:], p_y[t][:], ACT.Copy, scale=ga_t[:, t : t + 1])
            else:
                nc.vector.tensor_scalar(y_win[t][:], p_y[t][:], ga_t[:, t : t + 1], None, ALU.mult)
        for t in range(4):
            nc.vector.tensor_tensor(b_max[:, t, :], win[t][:, :V], b_got[:, t, :], ALU.max)
        z2_bf = tile("z2_bf", [P, V * 4], BF16)
        nc.vector.tensor_tensor(
            z2_bf[:].rearrange("p (c i t) -> p c t i", i=4, t=4),
            b_max[:].rearrange("p t (c i) -> p c t i", i=4),
            gb_t[:].rearrange("p (c t i) -> p c t i", c=1, i=1).to_broadcast([P, V // 4, 4, 4]),
            ALU.mult,
        )
        for t in range(4):
            fetch(d_got[t][:], d_win[t], l_n2, 0, S)
            for c in range(4):
                cols = slice(P * c, P * (c + 1))
                out = p_sum[c][:, P * t : P * (t + 1)]
                nc.tensor.matmul(out, d_got[t][:, cols], ident[:], start=True, stop=False, is_transpose=True)
                nc.tensor.matmul(out, d_win[t][:, cols], ident[:], start=False, stop=True, is_transpose=True)
        z2q = (tile("z2_words", [P, V], U32), tile("z2_scales", [P, V], U8))
        nc.vector.quantize_mx(out=z2q[0][:].bitcast(FP8X4), scales=z2q[1][:], in_=z2_bf[:])
        p_gate = [bank("p_gate%d" % c, 4 + c) for c in range(4)]

        def make_gate(c):
            nc.scalar.activation(
                gate_t[c][:].rearrange("p (t h b) -> p h t b", t=4, b=4),
                p_sum[c][:].rearrange("p (h t b) -> p h t b", t=4, b=4),
                ACT.Sigmoid,
            )
            for t in range(4):
                cols = slice(P * t, P * (t + 1))
                nc.tensor.transpose(p_gate[c][:, cols], gate_t[c][:, cols], ident[:])

        zq = (tile("z_words", [P, S], U32), tile("z_scales", [P, S], U8))
        z_bf = [tile("z_bf%d" % h, [P, 4 * 64 * 4], BF16) for h in range(2)]

        def y_fetch(lo, hi):
            for t in range(4):
                y_got = sb.tile([P, hi - lo], F32, name="y_got", tag="y_got%d" % t, align_bytes=64)
                fetch(y_got[:], y_win[t], l_n1, lo, hi)
                nc.vector.tensor_tensor(y_sum[:, t, lo:hi], y_win[t][:, lo:hi], y_got[:], ALU.add)
            return y_got

        def z_make(c, r0, r1):
            h, m0 = c // 2, c % 2 * 32
            nc.vector.tensor_tensor(
                z_bf[h][:].rearrange("p (r m t) -> p m t r", r=4, t=4)[:, m0 : m0 + 32, :, r0:r1],
                y_sum[:, :, P * c : P * (c + 1)].rearrange("p t (m r) -> p m t r", r=4)[:, :, :, r0:r1],
                p_gate[c][:].rearrange("p (t m r) -> p m t r", t=4, r=4)[:, :, :, r0:r1],
                ALU.mult,
            )

        def z_quantize(h, r):
            cols = slice(P * r + 64 * h, P * r + 64 * (h + 1))
            nc.vector.quantize_mx(
                out=zq[0][:, cols].bitcast(FP8X4), scales=zq[1][:, cols], in_=z_bf[h][:, 256 * r : 256 * (r + 1)]
            )

        for c in range(4):
            make_gate(c)
        cuts = (0,256,384,512)
        for lo, hi in zip(cuts, cuts[1:]):
            y_last = y_fetch(lo, hi)
            for c in range(lo // P, hi // P):
                if c < 3:
                    z_make(c, 0, 4)
                if c == 2:
                    for r in range(4):
                        z_quantize(0, r)
        z_make(3, 0, 2)
        z_make(3, 2, 4)
        nc.scalar.activation(warm[:, 0:1], y_last[:, 0:1], ACT.Abs_reciprocal_sqrt, bias=0.25, scale=0.5)
        p_s = [bank("p_s%d" % r, r) for r in range(4)]
        for r in range(4):
            z_quantize(1, r)
            product(p_s[r][:, :V], zq, r, z2q)
        for r in range(4):
            nc.vector.tensor_scalar(win[r][:, :V], p_s[r][:, :V], 0.0625, None, ALU.mult)

        out_words = tile("out_words", [P, V], U32)
        out_scales = tile("out_scales", [P, V], U8)
        out_rows = out_0.rearrange("(p r) v -> p r v", r=4)
        res = tile("res", [P, 4, V], F32)
        rounded = tile("rounded", [P, 4 * V], BF16)
        pieces = [(r, 0, V) for r in range(4)]
        held = {}

        def stage_fetch(k):
            r, lo, hi = pieces[k]
            pa = tile("pa%d" % k, [P, hi - lo], F32)
            pb = tile("pb%d" % k, [P, hi - lo], F32)
            fetch(pa[:], win[r], l_n4, lo, hi)
            fetch(pb[:], win[r], l_n5, lo, hi)
            held[k] = [pa, pb]

        def stage_linear(k):
            r, lo, hi = pieces[k]
            pa, pb = held[k]
            raw = p_s[r][:, lo:hi]
            both = tile("both%d" % k, [P, hi - lo], F32)
            fg = tile("fg%d" % k, [P, 2, hi - lo], F32)
            num = tile("num%d" % k, [P, hi - lo], F32)
            nc.vector.tensor_tensor(both[:], pa[:], pb[:], ALU.add)
            nc.vector.tensor_tensor(fg[:, 0], pa[:], pb[:], ALU.subtract)
            nc.vector.scalar_tensor_tensor(fg[:, 1], both[:], -9.6, raw, ALU.mult, ALU.add)
            nc.vector.scalar_tensor_tensor(num[:], both[:], -80.0 / 11.0, raw, ALU.mult, ALU.add)
            held[k] = [fg, num]

        def stage_square(k):
            fg, num = held[k]
            sq = tile("sq%d" % k, list(fg.shape), F32)
            if k in ():
                nc.vector.tensor_tensor(sq[:], fg[:], fg[:], ALU.mult)
            else:
                nc.scalar.activation(sq[:], fg[:], ACT.Square)
            held[k] = [sq, num]

        def stage_sum(k):
            sq, num = held[k]
            q = tile("q%d" % k, list(num.shape), F32)
            nc.vector.scalar_tensor_tensor(q[:], sq[:, 1], 0.390625 / 256.0, sq[:, 0], ALU.mult, ALU.add)
            held[k] = [q, num]

        def stage_root(k):
            q, num = held[k]
            inv = tile("inv%d" % k, list(num.shape), F32)
            nc.scalar.activation(inv[:], q[:], ACT.Abs_reciprocal_sqrt, bias=0.25, scale=0.5)
            held[k] = [inv, num]

        def stage_out(k):
            r, lo, hi = pieces[k]
            inv, num = held[k]
            nc.vector.scalar_tensor_tensor(res[:, r, lo:hi], num[:], 0.6875 / 16.0, inv[:], ALU.mult, ALU.mult)
            nc.sync.dma_start(out_rows[:, r, lo:hi], res[:, r, lo:hi])

        def stage_round(k):
            r, lo, hi = pieces[k]
            if r == 3:
                nc.vector.tensor_copy(
                    rounded[:, 4 * lo : 4 * hi].rearrange("p (c i r) -> p c r i", i=4, r=4),
                    res[:, :, lo:hi].rearrange("p r (c i) -> p c r i", i=4),
                )

        def stage_planes(k):
            r, lo, hi = pieces[k]
            if r == 3:
                nc.vector.quantize_mx(
                    out=out_words[:, lo:hi].bitcast(FP8X4), scales=out_scales[:, lo:hi], in_=rounded[:, 4 * lo : 4 * hi]
                )
                nc.sync.dma_start(
                    out_1[0].rearrange("p c r -> p (c r)").bitcast(I32)[:, lo:hi], out_words[:, lo:hi].bitcast(I32)
                )

        for k in range(len(pieces)):
            stage_fetch(k)
        for k in range(len(pieces)):
            stage_linear(k)
        stages = [stage_square, stage_sum, stage_root, stage_out, stage_round, stage_planes]
        for step in range(len(pieces) + len(stages) - 1):
            for depth in reversed(range(len(stages))):
                k = step - depth
                if 0 <= k < len(pieces):
                    stages[depth](k)
        for q in range(4):
            engine = nc.scalar if q % 2 else nc.sync
            engine.dma_start(
                out_2[0][4 * q : 4 * q + 4, :].bitcast(I32), out_scales[32 * q : 32 * q + 4, :].bitcast(I32)
            )
